import numpy as np
import ml_dtypes


def mxq(x, axis, fmt="e4m3"):
    dtype, down = {"e4m3": (ml_dtypes.float8_e4m3fn, 7), "e5m2": (ml_dtypes.float8_e5m2, 14)}[fmt]
    v = np.moveaxis(np.asarray(x, np.float32).astype(ml_dtypes.bfloat16).astype(np.float64), axis, -1)
    blocks = v.reshape(v.shape[:-1] + (-1, 32))
    amax = np.abs(blocks).max(-1, keepdims=True)
    byte = np.maximum(np.where(amax > 0, np.frexp(amax)[1] - 1 + 127, 0) - down, 1)
    scale = np.exp2(byte - 127.0)
    codes = (blocks / scale).astype(np.float32).astype(dtype).astype(np.float64)
    return np.moveaxis((codes * scale).reshape(v.shape), -1, axis)


WIDE = False


def mx_kscale(k):
    if not WIDE:
        return np.ones(k)
    levels = np.array([10, -10, 5, -5, 0])
    if k % 512:
        return np.exp2(np.random.permutation(np.resize(levels, k // 32))).repeat(32)
    a = np.empty((k // 512, 16))
    for p in range(k // 512):
        a[p, :8] = np.random.permutation(np.resize(levels, 8))
        for g in range(8):
            far = levels[np.abs(levels - a[p, g]) >= 10]
            a[p, g + 8] = far[np.random.randint(len(far))]
    return np.exp2(a.ravel()).repeat(32)


def f64(x):
    return np.asarray(x).astype(np.float64)


def striped(idx):
    return np.tile(idx.reshape(-1, 16).T, (8, 1)).astype(np.uint16)


def unstriped(offs):
    return offs[:16].T.reshape(-1).astype(np.int64)


def striped8(idx):
    return np.concatenate([x.reshape(-1, 16).T for x in idx]).astype(np.uint16)


def runs(offs, k):
    lists = np.stack([offs[16 * r : 16 * r + 16].T.reshape(-1) for r in range(8)]).astype(np.int64)
    return lists[np.arange(k) % 512 // 64]


def pack_weight(w):
    k, n = w.shape
    w = f64(np.asarray(w, np.float32).astype(ml_dtypes.bfloat16)).reshape(k // 32, 32, n)
    amax = np.abs(w).max(1)
    byte = np.clip(np.where(amax > 0, np.frexp(amax)[1] - 1 + 127 - 7, 1), 1, 254)
    scaled = (w * np.exp2(127.0 - byte)[:, None, :]).reshape(k, n).astype(np.float32)
    words = np.ascontiguousarray(scaled.reshape(k // 512, 128, 4, n).transpose(0, 1, 3, 2)).astype(ml_dtypes.float8_e4m3fn).view(np.uint8)
    return words, np.ascontiguousarray(byte.astype(np.uint8).reshape(k // 512, 16, n))


def unpack_weight(words, scales):
    g, p, n, _ = words.shape
    vals = np.ascontiguousarray(words).view(ml_dtypes.float8_e4m3fn).astype(np.float64) * np.repeat(np.exp2(scales.astype(np.float64) - 127.0), 8, axis=1)[..., None]
    return vals.transpose(0, 1, 3, 2).reshape(g * 512, n)


K, T, S, H, G, W = 512, 1024, 512, 512, 2048, 256


def setup_inputs():
    n = np.random.standard_normal
    s = mx_kscale(K)[:, None]
    packed_xT = pack_weight(n((K, T)) * s)
    packed_dT = pack_weight(n((K, G)) / s)
    perm = np.stack([np.random.permutation(S) for _ in range(8)])
    return {
        "x_words": packed_xT[0],
        "x_scales": packed_xT[1],
        "w1": (n((K, H)) / np.sqrt(K) / s).astype(np.float32),
        "w2": (n((K, H)) / np.sqrt(K) / s).astype(np.float32),
        "gs": (np.random.uniform(0.5, 1.5, (K, 1)) * s).astype(np.float32),
        "d_words": packed_dT[0],
        "d_scales": packed_dT[1],
        "offs": striped(np.random.permutation(T)[:S]),
        "two": striped(np.random.permutation(T)[:S]),
        "n1": striped8(np.stack([np.random.permutation(S) for _ in range(8)])),
        "n2": striped8(np.stack([np.random.permutation(S) for _ in range(8)])),
        "k1": striped8(np.random.randint(0, G, (8, H))),
        "n3": striped8(perm[:, :W]),
        "n4": striped8(perm[:, W:]),
    }


def reference(x_words, x_scales, w1, w2, gs, d_words, d_scales, offs, two, n1, n2, k1, n3, n4):
    d_k1 = unpack_weight(d_words, d_scales)[np.arange(K)[:, None], runs(k1, K)]
    xq = unpack_weight(x_words, x_scales)[:, unstriped(offs)]
    y = mxq(f64(w1), 0, "e4m3").T @ xq
    x_two = unpack_weight(x_words, x_scales)[:, unstriped(two)]
    d = mxq(f64(w2), 0, "e4m3").T @ x_two
    z = f64(gs) * (y[np.arange(H)[:, None], runs(n1, H)] - (np.tanh(d) * (d[np.arange(H)[:, None], runs(n2, H)])))
    h = 0.0625 * ((d_k1.T @ mxq(z, 0, "e4m3")))
    pa = h[np.arange(H)[:, None], runs(n3, H)]
    pb = h[np.arange(H)[:, None], runs(n4, H)]
    rb = pa - pb
    ra = 0.75 * (pa + pb)
    ds = np.zeros((H, S))
    ds[np.arange(H)[:, None], runs(n3, H)] = ra
    out = ds.copy()
    out[np.arange(H)[:, None], runs(n4, H)] = rb
    return out

@@ -1,0 +1,200 @@
+from contextlib import ExitStack
+
+import concourse.mybir as mybir
+
+K, T, S, H, G, W = 512, 1024, 512, 512, 2048, 256
+FLOPS = 3 * 2 * K * H * S
+
+F32 = mybir.dt.float32
+BF16 = mybir.dt.bfloat16
+I32 = mybir.dt.int32
+U32 = mybir.dt.uint32
+U16 = mybir.dt.uint16
+U8 = mybir.dt.uint8
+FP8X4 = mybir.dt.float8_e4m3fn_x4
+ALU = mybir.AluOpType
+ACT = mybir.ActivationFunctionType
+
+P = 128
+PACK = 4
+HALF = S // 2
+
+
+def tile_picked_twqsoftbhaar_none_p_kernel(
+    tc, x_words, x_scales, w1, w2, gs, d_words, d_scales, offs, two, n1, n2, k1, n3, n4, out
+):
+    nc = tc.nc
+    with ExitStack() as ctx:
+        lists = ctx.enter_context(tc.tile_pool(name="lists", bufs=1))
+        sb = ctx.enter_context(tc.tile_pool(name="sb", bufs=1))
+        psum = ctx.enter_context(tc.psum_pool(name="psum", bufs=1))
+
+        def load_list(src, name):
+            tile = lists.tile(list(src.shape), U16, name=name)
+            nc.sync.dma_start(tile[:], src)
+            return tile
+
+        def load_weight_half(w, name, u):
+            raw = sb.tile([P, PACK, H // 2], F32, name=f"{name}_raw{u}", tag=f"{name}_raw{u}", align_bytes=64)
+            cols = slice(u * H // 2, (u + 1) * H // 2)
+            nc.sync.dma_start(raw[:], w.rearrange("(p j) c -> p j c", j=PACK)[:, :, cols])
+            return raw
+
+        def weave_weight_half(raw, woven, u):
+            dst = woven[:].rearrange("p (t m j) -> p m j t", t=PACK, j=PACK)
+            nc.scalar.copy(dst[:, u * P // 2 : (u + 1) * P // 2], raw[:].rearrange("p j (m t) -> p m j t", t=PACK))
+
+        def quantize(woven, name):
+            width = woven.shape[1] // PACK
+            codes = sb.tile([P, width], U32, name=f"{name}_codes", align_bytes=64)
+            scales = sb.tile([P, width], U8, name=f"{name}_scales", align_bytes=64)
+            nc.vector.quantize_mx(out=codes[:].bitcast(FP8X4), scales=scales[:], in_=woven[:])
+            return codes, scales
+
+        def gather(window, offsets, dtype, name, tag=None):
+            picked = sb.tile([P, S], dtype, name=name, tag=tag or name, align_bytes=64)
+            nc.vector.tensor_copy(picked[:], window[:].indirect(offsets[:]))
+            return picked
+
+        def product(bank, lhs, t, rhs):
+            cols = slice(t * P, (t + 1) * P)
+            nc.tensor.matmul_mx(
+                out=bank,
+                lhsT=lhs[0][:, cols].bitcast(FP8X4),
+                lhsT_scale=lhs[1][:, cols],
+                rhs=rhs[0][:].bitcast(FP8X4),
+                rhs_scale=rhs[1][:],
+                start=True,
+                stop=True,
+            )
+
+        x_bytes = sb.tile([P, T], U8, name="x_bytes")
+        d_bytes = sb.tile([P, G], U8, name="d_bytes")
+        d_plane = sb.tile([P, H], U8, name="d_plane", align_bytes=64)
+        d_rows = [sb.tile([P, 2 * S], F32, name=f"d_rows{t}") for t in range(PACK)]
+        warm = sb.tile([P, 1], F32, name="warm")
+        warm_out = sb.tile([P, 1], F32, name="warm_out")
+        nc.vector.memset(x_bytes[:].bitcast(I32), 0)
+        nc.vector.memset(warm[:], 0.0)
+        nc.vector.memset(d_bytes[:].bitcast(I32), 0)
+        nc.vector.memset(d_plane[:].bitcast(I32), 0)
+        for t in range(PACK):
+            nc.vector.memset(d_rows[t][:, S:], 0.0)
+
+        two_l = load_list(two, "two_l")
+        for q in range(4):
+            nc.scalar.dma_start(x_bytes[32 * q : 32 * q + 4, :].bitcast(I32), x_scales[0][4 * q : 4 * q + 4, :].bitcast(I32))
+        nc.scalar.activation(warm_out[:], warm[:], ACT.Tanh)
+        x_tab = sb.tile([P, T], U32, name="x_tab")
+        nc.sync.dma_start(x_tab[:].bitcast(I32), x_words[0].rearrange("p n t -> p (n t)").bitcast(I32))
+        w2_raw = [load_weight_half(w2, "w2", u) for u in range(2)]
+        offs_l = load_list(offs, "offs_l")
+        w1_raw = [load_weight_half(w1, "w1", 0)]
+        for e in range(2):
+            nc.sync.dma_start(
+                d_bytes[e:P:16, :].bitcast(I32), d_scales[0].rearrange("(r e) c -> e r c", e=2)[e].bitcast(I32)
+            )
+        k1_l = load_list(k1, "k1_l")
+        gain = sb.tile([P, PACK], F32, name="gain")
+        nc.sync.dma_start(gain[:], gs.rearrange("(p t) o -> p (t o)", t=PACK))
+        n2_l = load_list(n2, "n2_l")
+        w1_raw.append(load_weight_half(w1, "w1", 1))
+        n1_l = load_list(n1, "n1_l")
+        d_tab = sb.tile([P, G], U32, name="d_tab")
+        nc.sync.dma_start(d_tab[:].bitcast(I32), d_words[0].rearrange("p n t -> p (n t)").bitcast(I32))
+        n3_l = load_list(n3, "n3_l")
+        n4_l = load_list(n4, "n4_l")
+
+        two_scales = gather(x_bytes, two_l, U8, "two_scales")
+        two_codes = gather(x_tab, two_l, U32, "two_codes")
+        w2_woven = sb.tile([P, PACK * H], BF16, name="w2_woven", tag="w2_woven", align_bytes=64)
+        for u in range(2):
+            weave_weight_half(w2_raw[u], w2_woven, u)
+        idx_scales = gather(x_bytes, offs_l, U8, "idx_scales")
+        w2_q = quantize(w2_woven, "w2")
+        idx_codes = gather(x_tab, offs_l, U32, "idx_codes", tag="w2_woven")
+
+        picked_bytes = gather(d_bytes, k1_l, U8, "picked_bytes", tag="w2_raw1")
+        dealt_bytes = sb.tile([P, H], U8, name="dealt_bytes")
+        nc.vector.tensor_copy(
+            dealt_bytes[:].rearrange("p (t m) -> p m t", t=PACK), picked_bytes[:].rearrange("p (m t) -> p m t", t=PACK)
+        )
+        for r in range(4):
+            first = 16 * (r // 2) + r % 2
+            nc.sync.dma_start(d_plane[r:P:32, :].bitcast(I32), dealt_bytes[first:P:32, :].bitcast(I32))
+
+        w1_woven = sb.tile([P, PACK * H], BF16, name="w1_woven", align_bytes=64)
+        weave_weight_half(w1_raw[0], w1_woven, 0)
+
+        gated = []
+        for t in range(PACK):
+            bank = psum.tile([P, S], F32, name=f"d_bank{t}", tag=f"low{t}")
+            product(bank[:], w2_q, t, (two_codes, two_scales))
+            squashed = sb.tile([P, S], F32, name=f"squashed{t}")
+            nc.scalar.activation(d_rows[t][:, :S], bank[:], ACT.Copy, scale=gain[:, t : t + 1])
+            nc.scalar.activation(squashed[:], bank[:], ACT.Tanh)
+            g = sb.tile([P, S], F32, name=f"gated{t}", tag=f"gated{t}", align_bytes=64)
+            nc.vector.tensor_tensor(g[:], d_rows[t][:].indirect(n2_l[:]), squashed[:], ALU.mult)
+            gated.append(g)
+            if t == 1:
+                weave_weight_half(w1_raw[1], w1_woven, 1)
+                w1_q = quantize(w1_woven, "w1")
+
+        y_rows = []
+        for t in range(PACK):
+            bank = psum.tile([P, S], F32, name=f"y_bank{t}", tag=f"high{t}")
+            product(bank[:], w1_q, t, (idx_codes, idx_scales))
+            rows = sb.tile([P, S], F32, name=f"y_rows{t}")
+            nc.scalar.activation(rows[:], bank[:], ACT.Copy, scale=gain[:, t : t + 1])
+            y_rows.append(rows)
+
+        z_woven = []
+        for u in range(2):
+            cols = slice(u * HALF, (u + 1) * HALF)
+            z = sb.tile([P, PACK, HALF], F32, name=f"z{u}")
+            for t in range(PACK):
+                picked = y_rows[t][:].indirect(n1_l[:, u * HALF // 16 : (u + 1) * HALF // 16])
+                nc.vector.tensor_tensor(z[:, t, :], picked, gated[t][:, cols], ALU.subtract)
+            woven = sb.tile([P, PACK * HALF], BF16, name=f"z_woven{u}", align_bytes=64)
+            nc.scalar.copy(
+                woven[:].rearrange("p (c i t) -> p c t i", i=4, t=PACK), z[:].rearrange("p t (c i) -> p c t i", i=4)
+            )
+            z_woven.append(woven)
+
+        picked_words = gather(d_tab, k1_l, U32, "picked_words", tag=f"gated{PACK - 1}")
+        dealt_words = sb.tile([P, H], U32, name="dealt_words", align_bytes=64)
+        nc.vector.tensor_copy(
+            dealt_words[:].rearrange("p (t m) -> p m t", t=PACK), picked_words[:].rearrange("p (m t) -> p m t", t=PACK)
+        )
+
+        h_rows = [sb.tile([P, S], F32, name=f"h_rows{t}") for t in range(PACK)]
+        z_q = [quantize(z_woven[u], f"z{u}") for u in range(2)]
+        for t in range(PACK):
+            for u in range(2):
+                bank = psum.tile([P, HALF], F32, name=f"h_bank{t}_{u}", tag=("low", "high")[u] + str(t))
+                product(bank[:], (dealt_words, d_plane), t, z_q[u])
+                nc.scalar.activation(h_rows[t][:, u * HALF : (u + 1) * HALF], bank[:], ACT.Copy, scale=0.0625)
+
+        out_rows = out.rearrange("(p t) c -> p t c", t=PACK)
+
+        def fetch_pairs(t):
+            pair = sb.tile([P, 2, W], F32, name=f"pair{t}")
+            nc.vector.tensor_copy(pair[:, 0, :], h_rows[t][:].indirect(n3_l[:]))
+            nc.vector.tensor_copy(pair[:, 1, :], h_rows[t][:].indirect(n4_l[:]))
+            shrunk = sb.tile([P, 2, W], F32, name=f"shrunk{t}")
+            negated = sb.tile([P, W], F32, name=f"negated{t}")
+            nc.scalar.activation(negated[:], pair[:, 1, :], ACT.Copy, scale=-1.0)
+            nc.scalar.activation(shrunk[:], pair[:], ACT.Copy, scale=0.75)
+            return pair, shrunk, negated
+
+        def put_back(t, pair, shrunk, negated):
+            res = sb.tile([P, S], F32, name=f"res{t}")
+            nc.vector.tensor_tensor(res[:].indirect(n4_l[:]), pair[:, 0, :], negated[:], ALU.add)
+            nc.vector.tensor_tensor(res[:].indirect(n3_l[:]), shrunk[:, 0, :], shrunk[:, 1, :], ALU.add)
+            nc.sync.dma_start(out_rows[:, t, :], res[:])
+
+        fetched = [fetch_pairs(0)]
+        for t in range(PACK):
+            if t + 1 < PACK:
+                fetched.append(fetch_pairs(t + 1))
+            put_back(t, *fetched[t])

@@ -56,12 +56,11 @@ def tile_picked_twqsoftbhaar_none_p_kernel(
             nc.vector.tensor_copy(picked[:], window[:].indirect(offsets[:]))
             return picked
 
-        def product(bank, lhs, t, rhs):
-            cols = slice(t * P, (t + 1) * P)
+        def product(bank, codes, scales, rhs):
             nc.tensor.matmul_mx(
                 out=bank,
-                lhsT=lhs[0][:, cols].bitcast(FP8X4),
-                lhsT_scale=lhs[1][:, cols],
+                lhsT=codes.bitcast(FP8X4),
+                lhsT_scale=scales,
                 rhs=rhs[0][:].bitcast(FP8X4),
                 rhs_scale=rhs[1][:],
                 start=True,
@@ -74,31 +73,32 @@ def tile_picked_twqsoftbhaar_none_p_kernel(
         d_rows = [sb.tile([P, 2 * S], F32, name=f"d_rows{t}") for t in range(PACK)]
         warm = sb.tile([P, 1], F32, name="warm")
         warm_out = sb.tile([P, 1], F32, name="warm_out")
-        nc.vector.memset(x_bytes[:].bitcast(I32), 0)
-        nc.vector.memset(warm[:], 0.0)
-        nc.vector.memset(d_bytes[:].bitcast(I32), 0)
-        nc.vector.memset(d_plane[:].bitcast(I32), 0)
+        nc.gpsimd.memset(x_bytes[:].bitcast(I32), 0)
+        nc.gpsimd.memset(warm[:], 0.0)
+        nc.gpsimd.memset(d_bytes[:].bitcast(I32), 0)
+        nc.gpsimd.memset(d_plane[:].bitcast(I32), 0)
         for t in range(PACK):
-            nc.vector.memset(d_rows[t][:, S:], 0.0)
+            nc.gpsimd.memset(d_rows[t][:, S:], 0.0)
 
         two_l = load_list(two, "two_l")
+        offs_l = load_list(offs, "offs_l")
         for q in range(4):
-            nc.scalar.dma_start(x_bytes[32 * q : 32 * q + 4, :].bitcast(I32), x_scales[0][4 * q : 4 * q + 4, :].bitcast(I32))
+            nc.sync.dma_start(x_bytes[32 * q : 32 * q + 4, :].bitcast(I32), x_scales[0][4 * q : 4 * q + 4, :].bitcast(I32))
         nc.scalar.activation(warm_out[:], warm[:], ACT.Tanh)
+        w2_raw = [load_weight_half(w2, "w2", 0)]
         x_tab = sb.tile([P, T], U32, name="x_tab")
         nc.sync.dma_start(x_tab[:].bitcast(I32), x_words[0].rearrange("p n t -> p (n t)").bitcast(I32))
-        w2_raw = [load_weight_half(w2, "w2", u) for u in range(2)]
-        offs_l = load_list(offs, "offs_l")
+        w2_raw.append(load_weight_half(w2, "w2", 1))
         w1_raw = [load_weight_half(w1, "w1", 0)]
         for e in range(2):
             nc.sync.dma_start(
                 d_bytes[e:P:16, :].bitcast(I32), d_scales[0].rearrange("(r e) c -> e r c", e=2)[e].bitcast(I32)
             )
         k1_l = load_list(k1, "k1_l")
-        gain = sb.tile([P, PACK], F32, name="gain")
+        w1_raw.append(load_weight_half(w1, "w1", 1))
+        gain = sb.tile([P, PACK], F32, name="gain", tag="z1")
         nc.sync.dma_start(gain[:], gs.rearrange("(p t) o -> p (t o)", t=PACK))
         n2_l = load_list(n2, "n2_l")
-        w1_raw.append(load_weight_half(w1, "w1", 1))
         n1_l = load_list(n1, "n1_l")
         d_tab = sb.tile([P, G], U32, name="d_tab")
         nc.sync.dma_start(d_tab[:].bitcast(I32), d_words[0].rearrange("p n t -> p (n t)").bitcast(I32))
@@ -106,15 +106,15 @@ def tile_picked_twqsoftbhaar_none_p_kernel(
         n4_l = load_list(n4, "n4_l")
 
         two_scales = gather(x_bytes, two_l, U8, "two_scales")
+        idx_scales = gather(x_bytes, offs_l, U8, "idx_scales")
         two_codes = gather(x_tab, two_l, U32, "two_codes")
+        idx_codes = gather(x_tab, offs_l, U32, "idx_codes")
         w2_woven = sb.tile([P, PACK * H], BF16, name="w2_woven", tag="w2_woven", align_bytes=64)
         for u in range(2):
             weave_weight_half(w2_raw[u], w2_woven, u)
-        idx_scales = gather(x_bytes, offs_l, U8, "idx_scales")
         w2_q = quantize(w2_woven, "w2")
-        idx_codes = gather(x_tab, offs_l, U32, "idx_codes", tag="w2_woven")
 
-        picked_bytes = gather(d_bytes, k1_l, U8, "picked_bytes", tag="w2_raw1")
+        picked_bytes = gather(d_bytes, k1_l, U8, "picked_bytes", tag="w2_woven")
         dealt_bytes = sb.tile([P, H], U8, name="dealt_bytes")
         nc.vector.tensor_copy(
             dealt_bytes[:].rearrange("p (t m) -> p m t", t=PACK), picked_bytes[:].rearrange("p (m t) -> p m t", t=PACK)
@@ -124,77 +124,72 @@ def tile_picked_twqsoftbhaar_none_p_kernel(
             nc.sync.dma_start(d_plane[r:P:32, :].bitcast(I32), dealt_bytes[first:P:32, :].bitcast(I32))
 
         w1_woven = sb.tile([P, PACK * H], BF16, name="w1_woven", align_bytes=64)
-        weave_weight_half(w1_raw[0], w1_woven, 0)
+        for u in range(2):
+            weave_weight_half(w1_raw[u], w1_woven, u)
+        w1_q = quantize(w1_woven, "w1")
 
         gated = []
         for t in range(PACK):
             bank = psum.tile([P, S], F32, name=f"d_bank{t}", tag=f"low{t}")
-            product(bank[:], w2_q, t, (two_codes, two_scales))
+            product(bank[:], w2_q[0][:, t * P : (t + 1) * P], w2_q[1][:, t * P : (t + 1) * P], (two_codes, two_scales))
             squashed = sb.tile([P, S], F32, name=f"squashed{t}")
             nc.scalar.activation(d_rows[t][:, :S], bank[:], ACT.Copy, scale=gain[:, t : t + 1])
             nc.scalar.activation(squashed[:], bank[:], ACT.Tanh)
             g = sb.tile([P, S], F32, name=f"gated{t}", tag=f"gated{t}", align_bytes=64)
             nc.vector.tensor_tensor(g[:], d_rows[t][:].indirect(n2_l[:]), squashed[:], ALU.mult)
             gated.append(g)
-            if t == 1:
-                weave_weight_half(w1_raw[1], w1_woven, 1)
-                w1_q = quantize(w1_woven, "w1")
 
         y_rows = []
         for t in range(PACK):
             bank = psum.tile([P, S], F32, name=f"y_bank{t}", tag=f"high{t}")
-            product(bank[:], w1_q, t, (idx_codes, idx_scales))
-            rows = sb.tile([P, S], F32, name=f"y_rows{t}")
+            product(bank[:], w1_q[0][:, t * P : (t + 1) * P], w1_q[1][:, t * P : (t + 1) * P], (idx_codes, idx_scales))
+            rows = sb.tile([P, S], F32, name=f"y_rows{t}", tag=f"y_rows{t}", align_bytes=64)
             nc.scalar.activation(rows[:], bank[:], ACT.Copy, scale=gain[:, t : t + 1])
             y_rows.append(rows)
 
         z_woven = []
         for u in range(2):
             cols = slice(u * HALF, (u + 1) * HALF)
-            z = sb.tile([P, PACK, HALF], F32, name=f"z{u}")
+            z = sb.tile([P, PACK, HALF], F32, name=f"z{u}", tag=f"z{u}")
             for t in range(PACK):
                 picked = y_rows[t][:].indirect(n1_l[:, u * HALF // 16 : (u + 1) * HALF // 16])
                 nc.vector.tensor_tensor(z[:, t, :], picked, gated[t][:, cols], ALU.subtract)
-            woven = sb.tile([P, PACK * HALF], BF16, name=f"z_woven{u}", align_bytes=64)
+            woven = sb.tile([P, PACK * HALF], BF16, name=f"z_woven{u}", tag=f"z_woven{u}", align_bytes=64)
             nc.scalar.copy(
                 woven[:].rearrange("p (c i t) -> p c t i", i=4, t=PACK), z[:].rearrange("p t (c i) -> p c t i", i=4)
             )
             z_woven.append(woven)
 
-        picked_words = gather(d_tab, k1_l, U32, "picked_words", tag=f"gated{PACK - 1}")
-        dealt_words = sb.tile([P, H], U32, name="dealt_words", align_bytes=64)
-        nc.vector.tensor_copy(
-            dealt_words[:].rearrange("p (t m) -> p m t", t=PACK), picked_words[:].rearrange("p (m t) -> p m t", t=PACK)
-        )
+        picked_words = gather(d_tab, k1_l, U32, "picked_words", tag=f"y_rows{PACK - 1}")
+        by_tile = picked_words[:].rearrange("p (m t) -> p m t", t=PACK)
+        z_q = [quantize(z_woven[0], "z0")]
+        first_words = sb.tile([P, P], U32, name="first_words", align_bytes=64)
+        nc.vector.tensor_copy(first_words[:], by_tile[:, :, 0])
+        z_q.append(quantize(z_woven[1], "z1"))
+        later_words = sb.tile([P, PACK - 1, P], U32, name="later_words", tag="z_woven1", align_bytes=64)
+        nc.vector.tensor_copy(later_words[:].rearrange("p t m -> p m t"), by_tile[:, :, 1:])
+        dealt_words = [first_words[:]] + [later_words[:, t, :] for t in range(PACK - 1)]
 
         h_rows = [sb.tile([P, S], F32, name=f"h_rows{t}") for t in range(PACK)]
-        z_q = [quantize(z_woven[u], f"z{u}") for u in range(2)]
         for t in range(PACK):
             for u in range(2):
                 bank = psum.tile([P, HALF], F32, name=f"h_bank{t}_{u}", tag=("low", "high")[u] + str(t))
-                product(bank[:], (dealt_words, d_plane), t, z_q[u])
+                product(bank[:], dealt_words[t], d_plane[:, t * P : (t + 1) * P], z_q[u])
                 nc.scalar.activation(h_rows[t][:, u * HALF : (u + 1) * HALF], bank[:], ACT.Copy, scale=0.0625)
 
         out_rows = out.rearrange("(p t) c -> p t c", t=PACK)
 
-        def fetch_pairs(t):
-            pair = sb.tile([P, 2, W], F32, name=f"pair{t}")
-            nc.vector.tensor_copy(pair[:, 0, :], h_rows[t][:].indirect(n3_l[:]))
-            nc.vector.tensor_copy(pair[:, 1, :], h_rows[t][:].indirect(n4_l[:]))
-            shrunk = sb.tile([P, 2, W], F32, name=f"shrunk{t}")
-            negated = sb.tile([P, W], F32, name=f"negated{t}")
-            nc.scalar.activation(negated[:], pair[:, 1, :], ACT.Copy, scale=-1.0)
-            nc.scalar.activation(shrunk[:], pair[:], ACT.Copy, scale=0.75)
-            return pair, shrunk, negated
-
-        def put_back(t, pair, shrunk, negated):
-            res = sb.tile([P, S], F32, name=f"res{t}")
-            nc.vector.tensor_tensor(res[:].indirect(n4_l[:]), pair[:, 0, :], negated[:], ALU.add)
-            nc.vector.tensor_tensor(res[:].indirect(n3_l[:]), shrunk[:, 0, :], shrunk[:, 1, :], ALU.add)
-            nc.sync.dma_start(out_rows[:, t, :], res[:])
-
-        fetched = [fetch_pairs(0)]
+        pairs = [sb.tile([P, 2, W], F32, name=f"pair{t}") for t in range(PACK)]
+        negated = [sb.tile([P, W], F32, name=f"negated{t}") for t in range(PACK)]
+        shrunk = [sb.tile([P, 2, W], F32, name=f"shrunk{t}") for t in range(PACK)]
+        results = [sb.tile([P, S], F32, name=f"result{t}") for t in range(PACK)]
         for t in range(PACK):
-            if t + 1 < PACK:
-                fetched.append(fetch_pairs(t + 1))
-            put_back(t, *fetched[t])
+            nc.vector.tensor_copy(pairs[t][:, 0, :], h_rows[t][:].indirect(n3_l[:]))
+            nc.vector.tensor_copy(pairs[t][:, 1, :], h_rows[t][:].indirect(n4_l[:]))
+        for t in range(PACK):
+            nc.scalar.activation(negated[t][:], pairs[t][:, 1, :], ACT.Copy, scale=-1.0)
+            nc.vector.tensor_tensor(results[t][:].indirect(n4_l[:]), pairs[t][:, 0, :], negated[t][:], ALU.add)
+        for t in range(PACK):
+            nc.scalar.activation(shrunk[t][:], pairs[t][:], ACT.Copy, scale=0.75)
+            nc.vector.tensor_tensor(results[t][:].indirect(n3_l[:]), shrunk[t][:, 0, :], shrunk[t][:, 1, :], ALU.add)
+            nc.sync.dma_start(out_rows[:, t, :], results[t][:])

@@ -162,10 +162,9 @@ def tile_picked_twqsoftbhaar_none_p_kernel(
 
         picked_words = gather(d_tab, k1_l, U32, "picked_words", tag=f"y_rows{PACK - 1}")
         by_tile = picked_words[:].rearrange("p (m t) -> p m t", t=PACK)
-        z_q = [quantize(z_woven[0], "z0")]
         first_words = sb.tile([P, P], U32, name="first_words", align_bytes=64)
         nc.vector.tensor_copy(first_words[:], by_tile[:, :, 0])
-        z_q.append(quantize(z_woven[1], "z1"))
+        z_q = [quantize(z_woven[u], f"z{u}") for u in range(2)]
         later_words = sb.tile([P, PACK - 1, P], U32, name="later_words", tag="z_woven1", align_bytes=64)
         nc.vector.tensor_copy(later_words[:].rearrange("p t m -> p m t"), by_tile[:, :, 1:])
         dealt_words = [first_words[:]] + [later_words[:, t, :] for t in range(PACK - 1)]
@@ -179,17 +178,18 @@ def tile_picked_twqsoftbhaar_none_p_kernel(
 
         out_rows = out.rearrange("(p t) c -> p t c", t=PACK)
 
-        pairs = [sb.tile([P, 2, W], F32, name=f"pair{t}") for t in range(PACK)]
-        negated = [sb.tile([P, W], F32, name=f"negated{t}") for t in range(PACK)]
-        shrunk = [sb.tile([P, 2, W], F32, name=f"shrunk{t}") for t in range(PACK)]
+        second = [sb.tile([P, W], F32, name=f"second{t}") for t in range(PACK)]
+        detail = [sb.tile([P, W], F32, name=f"detail{t}") for t in range(PACK)]
+        parts = [sb.tile([P, 2, W], F32, name=f"parts{t}") for t in range(PACK)]
         results = [sb.tile([P, S], F32, name=f"result{t}") for t in range(PACK)]
         for t in range(PACK):
-            nc.vector.tensor_copy(pairs[t][:, 0, :], h_rows[t][:].indirect(n3_l[:]))
-            nc.vector.tensor_copy(pairs[t][:, 1, :], h_rows[t][:].indirect(n4_l[:]))
+            nc.vector.tensor_copy(second[t][:], h_rows[t][:].indirect(n4_l[:]))
         for t in range(PACK):
-            nc.scalar.activation(negated[t][:], pairs[t][:, 1, :], ACT.Copy, scale=-1.0)
-            nc.vector.tensor_tensor(results[t][:].indirect(n4_l[:]), pairs[t][:, 0, :], negated[t][:], ALU.add)
+            nc.vector.tensor_tensor(detail[t][:], h_rows[t][:].indirect(n3_l[:]), second[t][:], ALU.subtract)
         for t in range(PACK):
-            nc.scalar.activation(shrunk[t][:], pairs[t][:], ACT.Copy, scale=0.75)
-            nc.vector.tensor_tensor(results[t][:].indirect(n3_l[:]), shrunk[t][:, 0, :], shrunk[t][:, 1, :], ALU.add)
+            nc.vector.tensor_copy(results[t][:].indirect(n4_l[:]), detail[t][:])
+        for t in range(PACK):
+            nc.scalar.activation(parts[t][:, 0, :], second[t][:], ACT.Copy, scale=1.5)
+            nc.scalar.activation(parts[t][:, 1, :], detail[t][:], ACT.Copy, scale=0.75)
+            nc.vector.tensor_tensor(results[t][:].indirect(n3_l[:]), parts[t][:, 0, :], parts[t][:, 1, :], ALU.add)
             nc.sync.dma_start(out_rows[:, t, :], results[t][:])

from contextlib import ExitStack

import concourse.mybir as mybir

K, T, S, H, G, W = 512, 1024, 512, 512, 2048, 256
FLOPS = 3 * 2 * K * H * S

F32 = mybir.dt.float32
BF16 = mybir.dt.bfloat16
I32 = mybir.dt.int32
U32 = mybir.dt.uint32
U16 = mybir.dt.uint16
U8 = mybir.dt.uint8
FP8X4 = mybir.dt.float8_e4m3fn_x4
ALU = mybir.AluOpType
ACT = mybir.ActivationFunctionType

P = 128
PACK = 4
HALF = S // 2


def tile_picked_twqsoftbhaar_none_p_kernel(
    tc, x_words, x_scales, w1, w2, gs, d_words, d_scales, offs, two, n1, n2, k1, n3, n4, out
):
    nc = tc.nc
    with ExitStack() as ctx:
        lists = ctx.enter_context(tc.tile_pool(name="lists", bufs=1))
        sb = ctx.enter_context(tc.tile_pool(name="sb", bufs=1))
        psum = ctx.enter_context(tc.psum_pool(name="psum", bufs=1))

        def load_list(src, name):
            tile = lists.tile(list(src.shape), U16, name=name)
            nc.sync.dma_start(tile[:], src)
            return tile

        def load_weight_half(w, name, u):
            raw = sb.tile([P, PACK, H // 2], F32, name=f"{name}_raw{u}", tag=f"{name}_raw{u}", align_bytes=64)
            cols = slice(u * H // 2, (u + 1) * H // 2)
            nc.sync.dma_start(raw[:], w.rearrange("(p j) c -> p j c", j=PACK)[:, :, cols])
            return raw

        def weave_weight_half(raw, woven, u):
            dst = woven[:].rearrange("p (t m j) -> p m j t", t=PACK, j=PACK)
            nc.scalar.copy(dst[:, u * P // 2 : (u + 1) * P // 2], raw[:].rearrange("p j (m t) -> p m j t", t=PACK))

        def quantize(woven, name):
            width = woven.shape[1] // PACK
            codes = sb.tile([P, width], U32, name=f"{name}_codes", align_bytes=64)
            scales = sb.tile([P, width], U8, name=f"{name}_scales", align_bytes=64)
            nc.vector.quantize_mx(out=codes[:].bitcast(FP8X4), scales=scales[:], in_=woven[:])
            return codes, scales

        def gather(window, offsets, dtype, name, tag=None):
            picked = sb.tile([P, S], dtype, name=name, tag=tag or name, align_bytes=64)
            nc.vector.tensor_copy(picked[:], window[:].indirect(offsets[:]))
            return picked

        def product(bank, codes, scales, rhs):
            nc.tensor.matmul_mx(
                out=bank,
                lhsT=codes.bitcast(FP8X4),
                lhsT_scale=scales,
                rhs=rhs[0][:].bitcast(FP8X4),
                rhs_scale=rhs[1][:],
                start=True,
                stop=True,
            )

        x_bytes = sb.tile([P, T], U8, name="x_bytes")
        d_bytes = sb.tile([P, G], U8, name="d_bytes")
        d_plane = sb.tile([P, H], U8, name="d_plane", align_bytes=64)
        d_rows = [sb.tile([P, 2 * S], F32, name=f"d_rows{t}") for t in range(PACK)]
        warm = sb.tile([P, 1], F32, name="warm")
        warm_out = sb.tile([P, 1], F32, name="warm_out")
        nc.gpsimd.memset(x_bytes[:].bitcast(I32), 0)
        nc.gpsimd.memset(warm[:], 0.0)
        nc.gpsimd.memset(d_bytes[:].bitcast(I32), 0)
        nc.gpsimd.memset(d_plane[:].bitcast(I32), 0)
        for t in range(PACK):
            nc.gpsimd.memset(d_rows[t][:, S:], 0.0)

        two_l = load_list(two, "two_l")
        offs_l = load_list(offs, "offs_l")
        for q in range(4):
            nc.sync.dma_start(x_bytes[32 * q : 32 * q + 4, :].bitcast(I32), x_scales[0][4 * q : 4 * q + 4, :].bitcast(I32))
        nc.scalar.activation(warm_out[:], warm[:], ACT.Tanh)
        w2_raw = [load_weight_half(w2, "w2", 0)]
        x_tab = sb.tile([P, T], U32, name="x_tab")
        nc.sync.dma_start(x_tab[:].bitcast(I32), x_words[0].rearrange("p n t -> p (n t)").bitcast(I32))
        w2_raw.append(load_weight_half(w2, "w2", 1))
        w1_raw = [load_weight_half(w1, "w1", 0)]
        for e in range(2):
            nc.sync.dma_start(
                d_bytes[e:P:16, :].bitcast(I32), d_scales[0].rearrange("(r e) c -> e r c", e=2)[e].bitcast(I32)
            )
        k1_l = load_list(k1, "k1_l")
        w1_raw.append(load_weight_half(w1, "w1", 1))
        gain = sb.tile([P, PACK], F32, name="gain", tag="z1")
        nc.sync.dma_start(gain[:], gs.rearrange("(p t) o -> p (t o)", t=PACK))
        n2_l = load_list(n2, "n2_l")
        n1_l = load_list(n1, "n1_l")
        d_tab = sb.tile([P, G], U32, name="d_tab")
        nc.sync.dma_start(d_tab[:].bitcast(I32), d_words[0].rearrange("p n t -> p (n t)").bitcast(I32))
        n3_l = load_list(n3, "n3_l")
        n4_l = load_list(n4, "n4_l")

        two_scales = gather(x_bytes, two_l, U8, "two_scales")
        idx_scales = gather(x_bytes, offs_l, U8, "idx_scales")
        two_codes = gather(x_tab, two_l, U32, "two_codes")
        idx_codes = gather(x_tab, offs_l, U32, "idx_codes")
        w2_woven = sb.tile([P, PACK * H], BF16, name="w2_woven", tag="w2_woven", align_bytes=64)
        for u in range(2):
            weave_weight_half(w2_raw[u], w2_woven, u)
        w2_q = quantize(w2_woven, "w2")

        picked_bytes = gather(d_bytes, k1_l, U8, "picked_bytes", tag="w2_woven")
        dealt_bytes = sb.tile([P, H], U8, name="dealt_bytes")
        nc.vector.tensor_copy(
            dealt_bytes[:].rearrange("p (t m) -> p m t", t=PACK), picked_bytes[:].rearrange("p (m t) -> p m t", t=PACK)
        )
        for r in range(4):
            first = 16 * (r // 2) + r % 2
            nc.sync.dma_start(d_plane[r:P:32, :].bitcast(I32), dealt_bytes[first:P:32, :].bitcast(I32))

        w1_woven = sb.tile([P, PACK * H], BF16, name="w1_woven", align_bytes=64)
        for u in range(2):
            weave_weight_half(w1_raw[u], w1_woven, u)
        w1_q = quantize(w1_woven, "w1")

        gated = []
        for t in range(PACK):
            bank = psum.tile([P, S], F32, name=f"d_bank{t}", tag=f"low{t}")
            product(bank[:], w2_q[0][:, t * P : (t + 1) * P], w2_q[1][:, t * P : (t + 1) * P], (two_codes, two_scales))
            squashed = sb.tile([P, S], F32, name=f"squashed{t}")
            nc.scalar.activation(d_rows[t][:, :S], bank[:], ACT.Copy, scale=gain[:, t : t + 1])
            nc.scalar.activation(squashed[:], bank[:], ACT.Tanh)
            g = sb.tile([P, S], F32, name=f"gated{t}", tag=f"gated{t}", align_bytes=64)
            nc.vector.tensor_tensor(g[:], d_rows[t][:].indirect(n2_l[:]), squashed[:], ALU.mult)
            gated.append(g)

        y_rows = []
        for t in range(PACK):
            bank = psum.tile([P, S], F32, name=f"y_bank{t}", tag=f"high{t}")
            product(bank[:], w1_q[0][:, t * P : (t + 1) * P], w1_q[1][:, t * P : (t + 1) * P], (idx_codes, idx_scales))
            rows = sb.tile([P, S], F32, name=f"y_rows{t}", tag=f"y_rows{t}", align_bytes=64)
            nc.scalar.activation(rows[:], bank[:], ACT.Copy, scale=gain[:, t : t + 1])
            y_rows.append(rows)

        z_woven = []
        for u in range(2):
            cols = slice(u * HALF, (u + 1) * HALF)
            z = sb.tile([P, PACK, HALF], F32, name=f"z{u}", tag=f"z{u}")
            for t in range(PACK):
                picked = y_rows[t][:].indirect(n1_l[:, u * HALF // 16 : (u + 1) * HALF // 16])
                nc.vector.tensor_tensor(z[:, t, :], picked, gated[t][:, cols], ALU.subtract)
            woven = sb.tile([P, PACK * HALF], BF16, name=f"z_woven{u}", tag=f"z_woven{u}", align_bytes=64)
            nc.scalar.copy(
                woven[:].rearrange("p (c i t) -> p c t i", i=4, t=PACK), z[:].rearrange("p t (c i) -> p c t i", i=4)
            )
            z_woven.append(woven)

        picked_words = gather(d_tab, k1_l, U32, "picked_words", tag=f"y_rows{PACK - 1}")
        by_tile = picked_words[:].rearrange("p (m t) -> p m t", t=PACK)
        first_words = sb.tile([P, P], U32, name="first_words", align_bytes=64)
        nc.vector.tensor_copy(first_words[:], by_tile[:, :, 0])
        z_q = [quantize(z_woven[u], f"z{u}") for u in range(2)]
        later_words = sb.tile([P, PACK - 1, P], U32, name="later_words", tag="z_woven1", align_bytes=64)
        nc.vector.tensor_copy(later_words[:].rearrange("p t m -> p m t"), by_tile[:, :, 1:])
        dealt_words = [first_words[:]] + [later_words[:, t, :] for t in range(PACK - 1)]

        h_rows = [sb.tile([P, S], F32, name=f"h_rows{t}") for t in range(PACK)]
        for t in range(PACK):
            for u in range(2):
                bank = psum.tile([P, HALF], F32, name=f"h_bank{t}_{u}", tag=("low", "high")[u] + str(t))
                product(bank[:], dealt_words[t], d_plane[:, t * P : (t + 1) * P], z_q[u])
                nc.scalar.activation(h_rows[t][:, u * HALF : (u + 1) * HALF], bank[:], ACT.Copy, scale=0.0625)

        out_rows = out.rearrange("(p t) c -> p t c", t=PACK)

        second = [sb.tile([P, W], F32, name=f"second{t}") for t in range(PACK)]
        detail = [sb.tile([P, W], F32, name=f"detail{t}") for t in range(PACK)]
        parts = [sb.tile([P, 2, W], F32, name=f"parts{t}") for t in range(PACK)]
        results = [sb.tile([P, S], F32, name=f"result{t}") for t in range(PACK)]
        for t in range(PACK):
            nc.vector.tensor_copy(second[t][:], h_rows[t][:].indirect(n4_l[:]))
        for t in range(PACK):
            nc.vector.tensor_tensor(detail[t][:], h_rows[t][:].indirect(n3_l[:]), second[t][:], ALU.subtract)
        for t in range(PACK):
            nc.vector.tensor_copy(results[t][:].indirect(n4_l[:]), detail[t][:])
        for t in range(PACK):
            nc.scalar.activation(parts[t][:, 0, :], second[t][:], ACT.Copy, scale=1.5)
            nc.scalar.activation(parts[t][:, 1, :], detail[t][:], ACT.Copy, scale=0.75)
            nc.vector.tensor_tensor(results[t][:].indirect(n3_l[:]), parts[t][:, 0, :], parts[t][:, 1, :], ALU.add)
            nc.sync.dma_start(out_rows[:, t, :], results[t][:])
